import numpy as np
CORES = [51,54,179,182]
N = 4
W = 1024
def setup_inputs(rng):
    amp = 0.5 + 1.5 * rng.random((2, N, 128, 1), dtype=np.float32)
    return {"u": amp[0] * rng.standard_normal((N, 128, W), dtype=np.float32), "b": amp[1] * rng.standard_normal((N, 128, W), dtype=np.float32)}
def setup_inputs_big(rng):
    d = setup_inputs(rng)
    for k in ("u", "b"): d[k] = (d[k].astype(np.float32) * 1024.0).astype(d[k].dtype)
    return d
def setup_inputs_small(rng):
    d = setup_inputs(rng)
    for k in ("u", "b"): d[k] = (d[k].astype(np.float32) * (1 / 1024.0)).astype(d[k].dtype)
    return d
def setup_inputs_apart(rng):
    d = setup_inputs(rng)
    f = (10.0 ** rng.permutation(np.linspace(-1.5, 1.5, N))).astype(np.float32).reshape(N, 1, 1)
    for k in ("u", "b"): d[k] = (d[k].astype(np.float32) * f).astype(d[k].dtype)
    return d
def reference(u, b):
    g = np.concatenate(list(u.astype(np.float64)), axis=1); bb = np.concatenate(list(b.astype(np.float64)), axis=1)
    p = np.concatenate([g[:, -2:], g, g[:, :2]], axis=1)
    n = 0.125 * (p[:, :-4] + p[:, 1:-3] + p[:, 3:-1] + p[:, 4:]) + 0.5 * bb
    d = n - g
    s = np.stack([(d ** 2).mean(axis=1), np.abs(d).max(axis=1)], axis=1)
    return {"y": np.stack([n[:, W * r:W * r + W] for r in range(N)]).astype(np.float32), "s": np.broadcast_to(s.astype(np.float32), (N, 128, 2))}

@@ -1,0 +1,341 @@
+import numpy as np
+from concourse.bass import DstId, RemoteDMATransfer
+from concourse.mybir import AluOpType
+
+W = 1024
+NR = 4
+NCH = 6
+NPC = 5
+
+SCRATCH = {
+    "U": ("sbuf", [128, W + 4], "float32"),
+    "B": ("sbuf", [128, W], "float32"),
+    "P": ("sbuf", [128, W + 4], "float32"),
+    "Y": ("sbuf", [128, W], "float32"),
+    "D": ("sbuf", [128, W], "float32"),
+    "SQ": ("sbuf", [128, W], "float32"),
+    "J": ("sbuf", [128, 128], "float32"),
+    "CN": ("sbuf", [128, 128], "float32"),
+    "CH": ("sbuf", [128, 128], "float32"),
+    "DF": ("sbuf", [128, 128], "float32"),
+    "E": ("sbuf", [128, 128], "float32"),
+    "IH": ("sbuf", [128, 128], "float32"),
+    "I8": ("sbuf", [128, 128], "float32"),
+    "HIS": ("sbuf", [128, 128], "float32"),
+    "LOS": ("sbuf", [128, 128], "float32"),
+    "SS": ("sbuf", [128, 128], "float32"),
+    "LO2": ("sbuf", [128, 64], "float32"),
+    "XW": ("sbuf", [128, 192], "float32"),
+    "SW": ("sbuf", [128, 128], "float32"),
+    "L": ("sbuf", [128, 16], "float32"),
+    "A2": ("sbuf", [128, 4], "float32"),
+    "M2": ("sbuf", [128, 4], "float32"),
+    "TT": ("sbuf", [128, 4], "float32"),
+    "CS": ("sbuf", [128, 4], "float32"),
+    "SO": ("sbuf", [128, 2], "float32"),
+    "pa": ("psum", [128, 512], "float32"),
+    "pb": ("psum", [128, 512], "float32"),
+}
+for _k in range(NCH):
+    SCRATCH["yp%d" % _k] = ("psum", [128, 512], "float32")
+
+SEMAPHORES = (["u%d" % i for i in range(NPC)] + ["b%d" % i for i in range(NPC)]
+              + ["p%d" % i for i in range(NCH)] + ["y%d" % i for i in range(NCH)] + ["c%d" % i for i in range(NCH)]
+              + ["v", "jr", "px", "ih", "i8", "sr", "hon", "hoff", "st", "ls", "so", "sd", "yst"])
+
+
+def _bits(m):
+    return [1 << i for i in range(m.bit_length()) if (m >> i) & 1]
+
+
+def _pieces(regions, margin):
+    owner = -np.ones(W, dtype=np.int64)
+    out = []
+    for (a, b) in regions:
+        lo, hi = max(0, a - margin), min(W, b + margin)
+        idx = np.nonzero(owner[lo:hi] < 0)[0]
+        s, e = lo + int(idx.min()), lo + int(idx.max()) + 1
+        assert e - s == len(idx)
+        owner[s:e] = len(out)
+        out.append((s, e))
+    assert (owner >= 0).all()
+    return out, owner
+
+
+def rank_program(g, core, T, topo):
+    rank = T.rank_of(core)
+    if rank is None:
+        return
+    V, PE, SY, SC = g.vector, g.tensor, g.sync, g.scalar
+    ADD, SUB, MUL, MAX, MIN = AluOpType.add, AluOpType.subtract, AluOpType.mult, AluOpType.max, AluOpType.min
+    sem = T.sem
+    cores = list(T.cores)
+    left, right = cores[(rank - 1) % NR], cores[(rank + 1) % NR]
+
+    def on_chip(c):
+        return topo.host(c) == topo.host(core) and topo.chip(c) == topo.chip(core)
+
+    off_left = not on_chip(left)
+    assert on_chip(left) != on_chip(right)
+    near, far = (right, left) if off_left else (left, right)
+
+    far_bits = _bits(topo.mask(core, far))
+    near_bits = [x for x in _bits(topo.mask(core, near)) if x not in far_bits][:4]
+    n_far, n_near = len(far_bits), len(near_bits)
+
+    if off_left:
+        ch = [(384, 640), (128, 384), (640, 896), (896, 1024), (64, 128), (0, 64)]
+        far_reg = (0, 128)
+    else:
+        ch = [(384, 640), (640, 896), (128, 384), (0, 128), (896, 960), (960, 1024)]
+        far_reg = (896, 1024)
+    upc, uown = _pieces([ch[0], far_reg, ch[3], ch[1], ch[2]], 2)
+    bpc, bown = _pieces([ch[0], ch[1], ch[2], ch[3], far_reg], 0)
+
+    seen = set()
+
+    def need(q, qn, name, val):
+        if (qn, name) not in seen:
+            q.wait_ge(sem[name], val)
+            seen.add((qn, name))
+
+    order = [("u", 0), ("b", 0), ("u", 1), ("u", 2), ("u", 3), ("b", 1), ("u", 4), ("b", 2), ("b", 3), ("b", 4)]
+    for i, (t, k) in enumerate(order):
+        q = SY if i % 2 == 0 else SC
+        if t == "u":
+            s, e = upc[k]
+            q.dma_start(T.U[:, s + 2:e + 2], T.u[:, s:e]).then_inc(sem["u%d" % k], 16)
+        else:
+            s, e = bpc[k]
+            q.dma_start(T.B[:, s:e], T.b[:, s:e]).then_inc(sem["b%d" % k], 16)
+
+    need(g, "g", "u%d" % uown[0], 16)
+    need(g, "g", "u%d" % uown[W - 1], 16)
+
+    def halo(dst_core, src, dst):
+        rid, pid = topo.addr(dst_core, core)
+        nearby = on_chip(dst_core)
+        return RemoteDMATransfer(dst_ids=[DstId(rid=rid, pnc=pid)], dma_engine_mask=sum(near_bits if nearby else far_bits),
+                                 remote_sem=sem["hon" if nearby else "hoff"], src=src, dst=dst)
+
+    g.remote_dma_fused([halo(left, T.U[:, 2:4], T.U[:, W + 2:W + 4]), halo(right, T.U[:, W:W + 2], T.U[:, 0:2])],
+                       local_sem=sem.ls)
+
+    nv, wv = [0], [0]
+
+    def vop(inst):
+        inst.then_inc(sem.v, 1)
+        nv[0] += 1
+
+    def vsync():
+        if wv[0] < nv[0]:
+            V.wait_ge(sem.v, nv[0])
+            wv[0] = nv[0]
+
+    def tt(out, a, b, op):
+        return V.tensor_tensor(out, a, b, op)
+
+    dp, hi, lo, S = T.pa[:, 0:128], T.pa[:, 128:256], T.pa[:, 256:384], T.pa[:, 384:512]
+    hi64, lo64 = T.pa[:, 0:64], T.pa[:, 64:128]
+    zero, cq, sqd = T.pb[:, 0:128], T.pb[:, 128:256], T.pb[:, 256:384]
+    S64, xn = T.pb[:, 384:448], T.pb[:, 448:512]
+
+    vop(V.memset(T.J[:, 0:1], 0.0))
+    n = 1
+    while n < 128:
+        vop(V.memset(T.CN[:, n:2 * n], float(n)))
+        n *= 2
+    vop(V.memset(T.CH[:, :], 0.5))
+    vop(V.memset(zero, 0.0))
+    vop(V.memset(cq, 0.25))
+    vop(V.memset(T.CS[:, 0:1], 1.0 / (NR * W)))
+    n = 1
+    while n < 128:
+        vsync()
+        inst = tt(T.J[:, n:2 * n], T.J[:, 0:n], T.CN[:, n:2 * n], ADD)
+        if 2 * n < 128:
+            vop(inst)
+        else:
+            inst.then_inc(sem.jr, 1)
+        n *= 2
+    px = T["yp%d" % (NCH - 1)][:, 0:128]
+    need(PE, "t", "jr", 1)
+    PE.matmul(px, T.J[0:2, :], T.CH[0:2, :], True, True).then_inc(sem.px, 1)
+    need(V, "v", "jr", 1)
+    need(V, "v", "px", 1)
+    vop(tt(T.DF[:, :], T.J[:, :], px, SUB))
+    vsync()
+    vop(tt(sqd, T.DF[:, :], T.DF[:, :], MUL))
+    vsync()
+    vop(tt(T.E[:, :], T.CH[:, :], sqd, SUB))
+    vsync()
+    tt(T.IH[:, :], T.E[:, :], zero, MAX).then_inc(sem.ih, 1)
+    need(V, "v", "ih", 1)
+    tt(T.I8[:, :], T.IH[:, :], cq, MUL).then_inc(sem.i8, 1)
+
+    pown = -np.ones(W + 3, dtype=np.int64)
+
+    def pair(k):
+        a, b = ch[k]
+        idx = np.nonzero(pown[a:b + 3] < 0)[0]
+        s, e = a + int(idx.min()), a + int(idx.max()) + 1
+        assert e - s == len(idx)
+        pown[s:e] = k
+        for pc in sorted(set(int(x) for x in uown[max(0, s - 2):min(W, e - 1)])):
+            need(V, "v", "u%d" % pc, 16)
+        if s < 2:
+            need(V, "v", "hoff" if off_left else "hon", n_far if off_left else n_near)
+        if e + 1 > W + 2:
+            need(V, "v", "hon" if off_left else "hoff", n_near if off_left else n_far)
+        tt(T.P[:, s:e], T.U[:, s:e], T.U[:, s + 1:e + 1], ADD).then_inc(sem["p%d" % k], 1)
+        yp = T["yp%d" % k][:, 0:b - a]
+        need(PE, "t", "ih", 1)
+        for pc in sorted(set(int(x) for x in bown[a:b])):
+            need(PE, "t", "b%d" % pc, 16)
+        PE.matmul(yp, T.IH[:, :], T.B[:, a:b], True, False)
+        need(PE, "t", "i8", 1)
+        for pk in sorted(set(int(x) for x in pown[a:b + 3])):
+            need(PE, "t", "p%d" % pk, 1)
+        PE.matmul(yp, T.I8[:, :], T.P[:, a:b], False, False)
+        PE.matmul(yp, T.I8[:, :], T.P[:, a + 3:b + 3], False, True).then_inc(sem["y%d" % k], 1)
+
+    def ycopy(k):
+        a, b = ch[k]
+        V.tensor_copy(T.Y[:, a:b], T["yp%d" % k][:, 0:b - a]).then_inc(sem["c%d" % k], 1)
+
+    def post(k):
+        a, b = ch[k]
+        yp = T["yp%d" % k][:, 0:b - a]
+        need(V, "v", "y%d" % k, 1)
+        if k < NCH - 1:
+            ycopy(k)
+        vop(tt(T.D[:, a:b], yp, T.U[:, a + 2:b + 2], SUB))
+        if k == 0:
+            m = a + 128
+            vop(tt(dp, yp[:, 0:128], T.U[:, a + 2:m + 2], SUB))
+            vsync()
+            vop(tt(S, dp, T.D[:, a:m], MUL))
+            vop(tt(T.SQ[:, m:b], T.D[:, m:b], T.D[:, m:b], MUL))
+            vop(tt(hi, dp, T.D[:, m:b], MAX))
+            vop(tt(lo, dp, T.D[:, m:b], MIN))
+            vsync()
+            vop(tt(S, S, T.SQ[:, m:b], ADD))
+        elif k < 3:
+            m = a + 128
+            vsync()
+            vop(tt(T.SQ[:, a:b], T.D[:, a:b], T.D[:, a:b], MUL))
+            vop(tt(hi, hi, T.D[:, a:m], MAX))
+            vop(tt(lo, lo, T.D[:, a:m], MIN))
+            vsync()
+            vop(tt(S, S, T.SQ[:, a:m], ADD))
+            vop(tt(hi, hi, T.D[:, m:b], MAX))
+            vop(tt(lo, lo, T.D[:, m:b], MIN))
+            vsync()
+            vop(tt(S, S, T.SQ[:, m:b], ADD))
+        elif k == 3:
+            vsync()
+            vop(tt(T.SQ[:, a:b], T.D[:, a:b], T.D[:, a:b], MUL))
+            vop(tt(T.HIS[:, :], hi, T.D[:, a:b], MAX))
+            vop(tt(T.LOS[:, :], lo, T.D[:, a:b], MIN))
+            vsync()
+            vop(tt(T.SS[:, :], S, T.SQ[:, a:b], ADD))
+            vop(tt(hi64, T.HIS[:, 0:64], T.HIS[:, 64:128], MAX))
+            vop(tt(lo64, T.LOS[:, 0:64], T.LOS[:, 64:128], MIN))
+            vsync()
+            vop(tt(S64, T.SS[:, 0:64], T.SS[:, 64:128], ADD))
+        elif k == 4:
+            vsync()
+            vop(tt(T.SQ[:, a:b], T.D[:, a:b], T.D[:, a:b], MUL))
+            vop(tt(hi64, hi64, T.D[:, a:b], MAX))
+            vop(tt(lo64, lo64, T.D[:, a:b], MIN))
+            vsync()
+            vop(tt(S64, S64, T.SQ[:, a:b], ADD))
+        else:
+            vsync()
+            vop(tt(T.SQ[:, a:b], T.D[:, a:b], T.D[:, a:b], MUL))
+            vop(tt(T.LO2[:, :], lo64, T.D[:, a:b], MIN))
+            vop(tt(T.XW[:, 0:64], hi64, T.D[:, a:b], MAX))
+            vsync()
+            vop(tt(xn, zero[:, 0:64], T.LO2[:, :], SUB))
+            vop(tt(T.SW[:, 0:64], S64, T.SQ[:, a:b], ADD))
+            vsync()
+            vop(tt(T.XW[:, 64:128], T.XW[:, 0:64], xn, MAX))
+            xo, so, sn = 64, 0, 64
+            xnn = 64
+            first = True
+            while xnn > 1 or sn > 1:
+                if not first:
+                    vsync()
+                if sn > 1:
+                    h = sn // 2
+                    inst = tt(T.L[:, 12:13] if h == 1 else T.SW[:, so + sn:so + sn + h],
+                              T.SW[:, so:so + h], T.SW[:, so + h:so + sn], ADD)
+                    if h == 1:
+                        inst.then_inc(sem.sr, 1)
+                    else:
+                        vop(inst)
+                    so, sn = so + sn, h
+                if not first and xnn > 1:
+                    h = xnn // 2
+                    inst = tt(T.L[:, 13:14] if h == 1 else T.XW[:, xo + xnn:xo + xnn + h],
+                              T.XW[:, xo:xo + h], T.XW[:, xo + h:xo + xnn], MAX)
+                    if h == 1:
+                        inst.then_inc(sem.sr, 1)
+                    else:
+                        vop(inst)
+                    xo, xnn = xo + xnn, h
+                first = False
+
+    pair(0)
+    pair(1)
+    post(0)
+    pair(2)
+    post(1)
+    pair(3)
+    post(2)
+    pair(4)
+    post(3)
+    pair(5)
+    post(4)
+    post(5)
+    ycopy(NCH - 1)
+
+    need(g, "g", "sr", 2)
+    others = [c for c in cores if c != core]
+    fars = [c for c in others if not on_chip(c)]
+    share = len(far_bits) // len(fars)
+    trs, n_st = [], 0
+    for c in others:
+        rid, pid = topo.addr(c, core)
+        if on_chip(c):
+            bits = near_bits
+        else:
+            i = fars.index(c)
+            bits = far_bits[i * share:(i + 1) * share]
+        slot = (rank - T.rank_of(c)) % NR - 1
+        trs.append(RemoteDMATransfer(dst_ids=[DstId(rid=rid, pnc=pid)], dma_engine_mask=sum(bits), remote_sem=sem.st,
+                                     src=T.L[:, 12:14], dst=T.L[:, 4 * slot:4 * slot + 2]))
+        n_st += len(bits)
+    g.remote_dma_fused(trs, local_sem=sem.ls)
+
+    need(V, "v", "sr", 2)
+    need(V, "v", "st", n_st)
+    vsync()
+    vop(tt(T.A2[:, 0:2], T.L[:, 0:16:8], T.L[:, 4:16:8], ADD))
+    vop(tt(T.M2[:, 0:2], T.L[:, 1:16:8], T.L[:, 5:16:8], MAX))
+    vsync()
+    vop(tt(T.TT[:, 0:1], T.A2[:, 0:1], T.A2[:, 1:2], ADD))
+    tt(T.SO[:, 1:2], T.M2[:, 0:1], T.M2[:, 1:2], MAX).then_inc(sem.so, 1)
+    vsync()
+    tt(T.SO[:, 0:1], T.TT[:, 0:1], T.CS[:, 0:1], MUL).then_inc(sem.so, 1)
+
+    for k in range(NCH):
+        a, b = ch[k]
+        need(SC, "a", "c%d" % k, 1)
+        SC.dma_start(T.y[:, a:b], T.Y[:, a:b]).then_inc(sem.yst, 16)
+    need(SY, "s", "so", 2)
+    SY.dma_start(T.s[:, :], T.SO[:, :]).then_inc(sem.sd, 16)
+
+    g.wait_ge(sem.ls, n_far + n_near + n_st)
+    g.wait_ge(sem.yst, 16 * NCH)
+    g.wait_ge(sem.sd, 16)

@@ -1,73 +1,53 @@
-import numpy as np
 from concourse.bass import DstId, RemoteDMATransfer
-from concourse.mybir import AluOpType
+from concourse.mybir import AluOpType, AxisListType, ActivationFunctionType
 
 W = 1024
 NR = 4
-NCH = 6
-NPC = 5
+HW = W // 2
+ZW = W + 8
+OW = W + 4
+ME = 32
+MAIN = (HW - ME) // 2
+
+CH = {"x": (MAIN, 2 * MAIN), "y": (HW + 4 + ME, HW + 4 + ME + MAIN), "z": (0, MAIN), "w": (HW + 4 + ME + MAIN, OW),
+      "e": (HW - ME, HW + 4 + ME)}
+POFF = {"x": 0, "y": 260, "z": 520, "w": 780, "e": 1040}
+UPC = {"uA": (MAIN, HW + 2, HW - 2 + MAIN), "uB": (HW + 6, HW + 8 + ME + MAIN, 0), "uC": (0, MAIN, HW - 2),
+       "uD": (HW + 8 + ME + MAIN, ZW, 2 + ME + MAIN)}
+BPC = {"bA": (MAIN, HW, HW + MAIN), "bB": (HW + 4, HW + 4 + ME + MAIN, 0), "bC": (0, MAIN, HW),
+       "bD": (HW + 4 + ME + MAIN, OW, ME + MAIN)}
+NPAIR = 6
 
 SCRATCH = {
-    "U": ("sbuf", [128, W + 4], "float32"),
-    "B": ("sbuf", [128, W], "float32"),
-    "P": ("sbuf", [128, W + 4], "float32"),
-    "Y": ("sbuf", [128, W], "float32"),
-    "D": ("sbuf", [128, W], "float32"),
-    "SQ": ("sbuf", [128, W], "float32"),
-    "J": ("sbuf", [128, 128], "float32"),
-    "CN": ("sbuf", [128, 128], "float32"),
-    "CH": ("sbuf", [128, 128], "float32"),
-    "DF": ("sbuf", [128, 128], "float32"),
-    "E": ("sbuf", [128, 128], "float32"),
-    "IH": ("sbuf", [128, 128], "float32"),
-    "I8": ("sbuf", [128, 128], "float32"),
-    "HIS": ("sbuf", [128, 128], "float32"),
-    "LOS": ("sbuf", [128, 128], "float32"),
-    "SS": ("sbuf", [128, 128], "float32"),
-    "LO2": ("sbuf", [128, 64], "float32"),
-    "XW": ("sbuf", [128, 192], "float32"),
-    "SW": ("sbuf", [128, 128], "float32"),
-    "L": ("sbuf", [128, 16], "float32"),
-    "A2": ("sbuf", [128, 4], "float32"),
-    "M2": ("sbuf", [128, 4], "float32"),
-    "TT": ("sbuf", [128, 4], "float32"),
-    "CS": ("sbuf", [128, 4], "float32"),
+    "Z": ("sbuf", [128, ZW], "float32"),
+    "B": ("sbuf", [128, OW], "float32"),
+    "P": ("sbuf", [128, 1120], "float32"),
+    "Y": ("sbuf", [128, OW], "float32"),
+    "D": ("sbuf", [128, OW], "float32"),
+    "SQ": ("sbuf", [128, OW], "float32"),
+    "L": ("sbuf", [128, 2 * NPAIR * NR], "float32"),
     "SO": ("sbuf", [128, 2], "float32"),
-    "pa": ("psum", [128, 512], "float32"),
-    "pb": ("psum", [128, 512], "float32"),
 }
-for _k in range(NCH):
-    SCRATCH["yp%d" % _k] = ("psum", [128, 512], "float32")
+for _k in "xyzw":
+    SCRATCH["pu" + _k] = ("psum", [128, 512], "float32")
+    SCRATCH["pq" + _k] = ("psum", [128, 512], "float32")
 
-SEMAPHORES = (["u%d" % i for i in range(NPC)] + ["b%d" % i for i in range(NPC)]
-              + ["p%d" % i for i in range(NCH)] + ["y%d" % i for i in range(NCH)] + ["c%d" % i for i in range(NCH)]
-              + ["v", "jr", "px", "ih", "i8", "sr", "hon", "hoff", "st", "ls", "so", "sd", "yst"])
+SEMAPHORES = ([s + k for k in "xyzwe" for s in ("a1", "v1", "a2", "v2", "a3", "v3", "a4", "v4")]
+              + list(UPC) + list(BPC) + ["bz", "hl", "hr", "sr", "st", "ls", "so", "sd", "yst"])
 
 
 def _bits(m):
     return [1 << i for i in range(m.bit_length()) if (m >> i) & 1]
 
 
-def _pieces(regions, margin):
-    owner = -np.ones(W, dtype=np.int64)
-    out = []
-    for (a, b) in regions:
-        lo, hi = max(0, a - margin), min(W, b + margin)
-        idx = np.nonzero(owner[lo:hi] < 0)[0]
-        s, e = lo + int(idx.min()), lo + int(idx.max()) + 1
-        assert e - s == len(idx)
-        owner[s:e] = len(out)
-        out.append((s, e))
-    assert (owner >= 0).all()
-    return out, owner
-
-
 def rank_program(g, core, T, topo):
     rank = T.rank_of(core)
     if rank is None:
         return
-    V, PE, SY, SC = g.vector, g.tensor, g.sync, g.scalar
-    ADD, SUB, MUL, MAX, MIN = AluOpType.add, AluOpType.subtract, AluOpType.mult, AluOpType.max, AluOpType.min
+    V, A, SY = g.vector, g.scalar, g.sync
+    ADD, SUB, MAX = AluOpType.add, AluOpType.subtract, AluOpType.max
+    COPY, SQUARE = ActivationFunctionType.Copy, ActivationFunctionType.Square
+    X = AxisListType.X
     sem = T.sem
     cores = list(T.cores)
     left, right = cores[(rank - 1) % NR], cores[(rank + 1) % NR]
@@ -75,232 +55,143 @@ def rank_program(g, core, T, topo):
     def on_chip(c):
         return topo.host(c) == topo.host(core) and topo.chip(c) == topo.chip(core)
 
-    off_left = not on_chip(left)
     assert on_chip(left) != on_chip(right)
-    near, far = (right, left) if off_left else (left, right)
+    near, far = (left, right) if on_chip(left) else (right, left)
 
     far_bits = _bits(topo.mask(core, far))
     near_bits = [x for x in _bits(topo.mask(core, near)) if x not in far_bits][:4]
     n_far, n_near = len(far_bits), len(near_bits)
 
-    if off_left:
-        ch = [(384, 640), (128, 384), (640, 896), (896, 1024), (64, 128), (0, 64)]
-        far_reg = (0, 128)
-    else:
-        ch = [(384, 640), (640, 896), (128, 384), (0, 128), (896, 960), (960, 1024)]
-        far_reg = (896, 1024)
-    upc, uown = _pieces([ch[0], far_reg, ch[3], ch[1], ch[2]], 2)
-    bpc, bown = _pieces([ch[0], ch[1], ch[2], ch[3], far_reg], 0)
-
     seen = set()
 
-    def need(q, qn, name, val):
+    def need(q, qn, name, val=1):
         if (qn, name) not in seen:
             q.wait_ge(sem[name], val)
             seen.add((qn, name))
 
-    order = [("u", 0), ("b", 0), ("u", 1), ("u", 2), ("u", 3), ("b", 1), ("u", 4), ("b", 2), ("b", 3), ("b", 4)]
-    for i, (t, k) in enumerate(order):
-        q = SY if i % 2 == 0 else SC
-        if t == "u":
-            s, e = upc[k]
-            q.dma_start(T.U[:, s + 2:e + 2], T.u[:, s:e]).then_inc(sem["u%d" % k], 16)
+    def need_z(q, qn, lo, hi):
+        for nm, (s, e, _) in UPC.items():
+            if s < hi and lo < e:
+                need(q, qn, nm, 16)
+        if HW + 2 < hi and lo < HW + 4:
+            need(q, qn, "hr", n_near if on_chip(right) else n_far)
+        if HW + 4 < hi and lo < HW + 6:
+            need(q, qn, "hl", n_near if on_chip(left) else n_far)
+
+    def need_b(q, qn, lo, hi):
+        for nm, (s, e, _) in BPC.items():
+            if s < hi and lo < e:
+                need(q, qn, nm, 16)
+        if HW < hi and lo < HW + 4:
+            need(q, qn, "bz", 1)
+
+    for i, nm in enumerate(["uA", "uB", "bA", "bB", "uC", "uD", "bC", "bD"]):
+        q = SY if i % 2 == 0 else A
+        if nm in UPC:
+            s, e, h = UPC[nm]
+            q.dma_start(T.Z[:, s:e], T.u[:, h:h + e - s]).then_inc(sem[nm], 16)
         else:
-            s, e = bpc[k]
-            q.dma_start(T.B[:, s:e], T.b[:, s:e]).then_inc(sem["b%d" % k], 16)
+            s, e, h = BPC[nm]
+            q.dma_start(T.B[:, s:e], T.b[:, h:h + e - s]).then_inc(sem[nm], 16)
+    V.memset(T.B[:, HW:HW + 4], 0.0).then_inc(sem.bz, 1)
 
-    need(g, "g", "u%d" % uown[0], 16)
-    need(g, "g", "u%d" % uown[W - 1], 16)
+    need(g, "g", "uA", 16)
+    need(g, "g", "uB", 16)
 
-    def halo(dst_core, src, dst):
+    def halo(dst_core, src, dst, name):
         rid, pid = topo.addr(dst_core, core)
-        nearby = on_chip(dst_core)
-        return RemoteDMATransfer(dst_ids=[DstId(rid=rid, pnc=pid)], dma_engine_mask=sum(near_bits if nearby else far_bits),
-                                 remote_sem=sem["hon" if nearby else "hoff"], src=src, dst=dst)
+        return RemoteDMATransfer(dst_ids=[DstId(rid=rid, pnc=pid)],
+                                 dma_engine_mask=sum(near_bits if on_chip(dst_core) else far_bits),
+                                 remote_sem=sem[name], src=src, dst=dst)
 
-    g.remote_dma_fused([halo(left, T.U[:, 2:4], T.U[:, W + 2:W + 4]), halo(right, T.U[:, W:W + 2], T.U[:, 0:2])],
+    g.remote_dma_fused([halo(left, T.Z[:, HW + 6:HW + 8], T.Z[:, HW + 2:HW + 4], "hr"),
+                        halo(right, T.Z[:, HW:HW + 2], T.Z[:, HW + 4:HW + 6], "hl")],
                        local_sem=sem.ls)
 
-    nv, wv = [0], [0]
-
-    def vop(inst):
-        inst.then_inc(sem.v, 1)
-        nv[0] += 1
-
-    def vsync():
-        if wv[0] < nv[0]:
-            V.wait_ge(sem.v, nv[0])
-            wv[0] = nv[0]
-
-    def tt(out, a, b, op):
-        return V.tensor_tensor(out, a, b, op)
-
-    dp, hi, lo, S = T.pa[:, 0:128], T.pa[:, 128:256], T.pa[:, 256:384], T.pa[:, 384:512]
-    hi64, lo64 = T.pa[:, 0:64], T.pa[:, 64:128]
-    zero, cq, sqd = T.pb[:, 0:128], T.pb[:, 128:256], T.pb[:, 256:384]
-    S64, xn = T.pb[:, 384:448], T.pb[:, 448:512]
-
-    vop(V.memset(T.J[:, 0:1], 0.0))
-    n = 1
-    while n < 128:
-        vop(V.memset(T.CN[:, n:2 * n], float(n)))
-        n *= 2
-    vop(V.memset(T.CH[:, :], 0.5))
-    vop(V.memset(zero, 0.0))
-    vop(V.memset(cq, 0.25))
-    vop(V.memset(T.CS[:, 0:1], 1.0 / (NR * W)))
-    n = 1
-    while n < 128:
-        vsync()
-        inst = tt(T.J[:, n:2 * n], T.J[:, 0:n], T.CN[:, n:2 * n], ADD)
-        if 2 * n < 128:
-            vop(inst)
+    def regs(k):
+        a, b = CH[k]
+        n = b - a
+        if k == "e":
+            up, pp, tw = T.pux[:, 264:264 + n + 3], T.pux[:, 336:336 + n], T.pux[:, 408:408 + n]
         else:
-            inst.then_inc(sem.jr, 1)
-        n *= 2
-    px = T["yp%d" % (NCH - 1)][:, 0:128]
-    need(PE, "t", "jr", 1)
-    PE.matmul(px, T.J[0:2, :], T.CH[0:2, :], True, True).then_inc(sem.px, 1)
-    need(V, "v", "jr", 1)
-    need(V, "v", "px", 1)
-    vop(tt(T.DF[:, :], T.J[:, :], px, SUB))
-    vsync()
-    vop(tt(sqd, T.DF[:, :], T.DF[:, :], MUL))
-    vsync()
-    vop(tt(T.E[:, :], T.CH[:, :], sqd, SUB))
-    vsync()
-    tt(T.IH[:, :], T.E[:, :], zero, MAX).then_inc(sem.ih, 1)
-    need(V, "v", "ih", 1)
-    tt(T.I8[:, :], T.IH[:, :], cq, MUL).then_inc(sem.i8, 1)
+            up, pp, tw = T["pu" + k][:, 0:n + 3], T["pq" + k][:, 0:n], T["pq" + k][:, 256:256 + n]
+        return a, b, n, up, pp, tw, POFF[k]
 
-    pown = -np.ones(W + 3, dtype=np.int64)
+    def a1(k):
+        a, b, n, up, pp, tw, po = regs(k)
+        need_z(A, "a", a, a + n + 3)
+        if k == "e":
+            need(A, "a", "v1x")
+            need(A, "a", "v4x")
+        A.activation(up, T.Z[:, a:a + n + 3], COPY).then_inc(sem["a1" + k], 1)
 
-    def pair(k):
-        a, b = ch[k]
-        idx = np.nonzero(pown[a:b + 3] < 0)[0]
-        s, e = a + int(idx.min()), a + int(idx.max()) + 1
-        assert e - s == len(idx)
-        pown[s:e] = k
-        for pc in sorted(set(int(x) for x in uown[max(0, s - 2):min(W, e - 1)])):
-            need(V, "v", "u%d" % pc, 16)
-        if s < 2:
-            need(V, "v", "hoff" if off_left else "hon", n_far if off_left else n_near)
-        if e + 1 > W + 2:
-            need(V, "v", "hon" if off_left else "hoff", n_near if off_left else n_far)
-        tt(T.P[:, s:e], T.U[:, s:e], T.U[:, s + 1:e + 1], ADD).then_inc(sem["p%d" % k], 1)
-        yp = T["yp%d" % k][:, 0:b - a]
-        need(PE, "t", "ih", 1)
-        for pc in sorted(set(int(x) for x in bown[a:b])):
-            need(PE, "t", "b%d" % pc, 16)
-        PE.matmul(yp, T.IH[:, :], T.B[:, a:b], True, False)
-        need(PE, "t", "i8", 1)
-        for pk in sorted(set(int(x) for x in pown[a:b + 3])):
-            need(PE, "t", "p%d" % pk, 1)
-        PE.matmul(yp, T.I8[:, :], T.P[:, a:b], False, False)
-        PE.matmul(yp, T.I8[:, :], T.P[:, a + 3:b + 3], False, True).then_inc(sem["y%d" % k], 1)
+    def v1(k):
+        a, b, n, up, pp, tw, po = regs(k)
+        need(V, "v", "a1" + k)
+        need_z(V, "v", a + 1, a + n + 4)
+        V.tensor_tensor(T.P[:, po:po + n + 3], up, T.Z[:, a + 1:a + n + 4], ADD).then_inc(sem["v1" + k], 1)
 
-    def ycopy(k):
-        a, b = ch[k]
-        V.tensor_copy(T.Y[:, a:b], T["yp%d" % k][:, 0:b - a]).then_inc(sem["c%d" % k], 1)
+    def a2(k):
+        a, b, n, up, pp, tw, po = regs(k)
+        need(A, "a", "v1" + k)
+        A.activation(pp, T.P[:, po:po + n], COPY).then_inc(sem["a2" + k], 1)
 
-    def post(k):
-        a, b = ch[k]
-        yp = T["yp%d" % k][:, 0:b - a]
-        need(V, "v", "y%d" % k, 1)
-        if k < NCH - 1:
-            ycopy(k)
-        vop(tt(T.D[:, a:b], yp, T.U[:, a + 2:b + 2], SUB))
-        if k == 0:
-            m = a + 128
-            vop(tt(dp, yp[:, 0:128], T.U[:, a + 2:m + 2], SUB))
-            vsync()
-            vop(tt(S, dp, T.D[:, a:m], MUL))
-            vop(tt(T.SQ[:, m:b], T.D[:, m:b], T.D[:, m:b], MUL))
-            vop(tt(hi, dp, T.D[:, m:b], MAX))
-            vop(tt(lo, dp, T.D[:, m:b], MIN))
-            vsync()
-            vop(tt(S, S, T.SQ[:, m:b], ADD))
-        elif k < 3:
-            m = a + 128
-            vsync()
-            vop(tt(T.SQ[:, a:b], T.D[:, a:b], T.D[:, a:b], MUL))
-            vop(tt(hi, hi, T.D[:, a:m], MAX))
-            vop(tt(lo, lo, T.D[:, a:m], MIN))
-            vsync()
-            vop(tt(S, S, T.SQ[:, a:m], ADD))
-            vop(tt(hi, hi, T.D[:, m:b], MAX))
-            vop(tt(lo, lo, T.D[:, m:b], MIN))
-            vsync()
-            vop(tt(S, S, T.SQ[:, m:b], ADD))
-        elif k == 3:
-            vsync()
-            vop(tt(T.SQ[:, a:b], T.D[:, a:b], T.D[:, a:b], MUL))
-            vop(tt(T.HIS[:, :], hi, T.D[:, a:b], MAX))
-            vop(tt(T.LOS[:, :], lo, T.D[:, a:b], MIN))
-            vsync()
-            vop(tt(T.SS[:, :], S, T.SQ[:, a:b], ADD))
-            vop(tt(hi64, T.HIS[:, 0:64], T.HIS[:, 64:128], MAX))
-            vop(tt(lo64, T.LOS[:, 0:64], T.LOS[:, 64:128], MIN))
-            vsync()
-            vop(tt(S64, T.SS[:, 0:64], T.SS[:, 64:128], ADD))
-        elif k == 4:
-            vsync()
-            vop(tt(T.SQ[:, a:b], T.D[:, a:b], T.D[:, a:b], MUL))
-            vop(tt(hi64, hi64, T.D[:, a:b], MAX))
-            vop(tt(lo64, lo64, T.D[:, a:b], MIN))
-            vsync()
-            vop(tt(S64, S64, T.SQ[:, a:b], ADD))
-        else:
-            vsync()
-            vop(tt(T.SQ[:, a:b], T.D[:, a:b], T.D[:, a:b], MUL))
-            vop(tt(T.LO2[:, :], lo64, T.D[:, a:b], MIN))
-            vop(tt(T.XW[:, 0:64], hi64, T.D[:, a:b], MAX))
-            vsync()
-            vop(tt(xn, zero[:, 0:64], T.LO2[:, :], SUB))
-            vop(tt(T.SW[:, 0:64], S64, T.SQ[:, a:b], ADD))
-            vsync()
-            vop(tt(T.XW[:, 64:128], T.XW[:, 0:64], xn, MAX))
-            xo, so, sn = 64, 0, 64
-            xnn = 64
-            first = True
-            while xnn > 1 or sn > 1:
-                if not first:
-                    vsync()
-                if sn > 1:
-                    h = sn // 2
-                    inst = tt(T.L[:, 12:13] if h == 1 else T.SW[:, so + sn:so + sn + h],
-                              T.SW[:, so:so + h], T.SW[:, so + h:so + sn], ADD)
-                    if h == 1:
-                        inst.then_inc(sem.sr, 1)
-                    else:
-                        vop(inst)
-                    so, sn = so + sn, h
-                if not first and xnn > 1:
-                    h = xnn // 2
-                    inst = tt(T.L[:, 13:14] if h == 1 else T.XW[:, xo + xnn:xo + xnn + h],
-                              T.XW[:, xo:xo + h], T.XW[:, xo + h:xo + xnn], MAX)
-                    if h == 1:
-                        inst.then_inc(sem.sr, 1)
-                    else:
-                        vop(inst)
-                    xo, xnn = xo + xnn, h
-                first = False
+    def v2(k):
+        a, b, n, up, pp, tw, po = regs(k)
+        need(V, "v", "v1" + k)
+        need(V, "v", "a2" + k)
+        V.tensor_tensor(tw, pp, T.P[:, po + 3:po + n + 3], ADD).then_inc(sem["v2" + k], 1)
 
-    pair(0)
-    pair(1)
-    post(0)
-    pair(2)
-    post(1)
-    pair(3)
-    post(2)
-    pair(4)
-    post(3)
-    pair(5)
-    post(4)
-    post(5)
-    ycopy(NCH - 1)
+    def a3(k):
+        a, b, n, up, pp, tw, po = regs(k)
+        need_b(A, "a", a, b)
+        A.activation(T.B[:, a:b], T.B[:, a:b], COPY, scale=4.0).then_inc(sem["a3" + k], 1)
 
-    need(g, "g", "sr", 2)
+    def v3(k):
+        a, b, n, up, pp, tw, po = regs(k)
+        need(V, "v", "v2" + k)
+        need(V, "v", "a3" + k)
+        V.tensor_tensor(tw, tw, T.B[:, a:b], ADD).then_inc(sem["v3" + k], 1)
+
+    def a4(k):
+        a, b, n, up, pp, tw, po = regs(k)
+        need(A, "a", "v3" + k)
+        A.activation(T.Y[:, a:b], tw, COPY, scale=0.125).then_inc(sem["a4" + k], 1)
+
+    def v4(k):
+        a, b, n, up, pp, tw, po = regs(k)
+        need(V, "v", "a4" + k)
+        V.tensor_tensor(T.D[:, a:b], T.Y[:, a:b], up[:, 2:n + 2], SUB).then_inc(sem["v4" + k], 1)
+
+    parts = {"x": [(CH["x"], 0)], "y": [(CH["y"], 1)], "z": [(CH["z"], 2)], "w": [(CH["w"], 3)],
+             "e": [((HW - ME, HW), 4), ((HW + 4, HW + 4 + ME), 5)]}
+    slot = 2 * NPAIR * rank
+
+    def a6(k):
+        need(A, "a", "v4" + k)
+        for (s, e), j in parts[k]:
+            c = slot + 2 * j
+            A.activation(T.SQ[:, s:e], T.D[:, s:e], SQUARE, scale=1.0 / 64.0,
+                         accum_out=T.L[:, c:c + 1]).then_inc(sem.sr, 1)
+
+    def v5(k):
+        need(V, "v", "v4" + k)
+        for (s, e), j in parts[k]:
+            c = slot + 2 * j + 1
+            V.tensor_reduce(T.L[:, c:c + 1], T.D[:, s:e], X, MAX, apply_absolute_value=True).then_inc(sem.sr, 1)
+
+    for f, k in [(a1, "x"), (a1, "y"), (a2, "x"), (a2, "y"), (a3, "x"), (a3, "y"), (a3, "e"), (a4, "x"), (a4, "y"),
+                 (a6, "x"), (a6, "y"),
+                 (a1, "z"), (a1, "w"), (a2, "z"), (a2, "w"), (a3, "z"), (a3, "w"), (a4, "z"), (a4, "w"),
+                 (a1, "e"), (a6, "z"), (a2, "e"), (a6, "w"), (a4, "e"), (a6, "e")]:
+        f(k)
+    for f, k in [(v1, "x"), (v1, "y"), (v2, "x"), (v2, "y"), (v3, "x"), (v3, "y"), (v4, "x"), (v4, "y"),
+                 (v5, "x"), (v5, "y"),
+                 (v1, "z"), (v1, "w"), (v2, "z"), (v2, "w"), (v3, "z"), (v3, "w"), (v4, "z"), (v4, "w"),
+                 (v1, "e"), (v5, "z"), (v2, "e"), (v3, "e"), (v5, "w"), (v4, "e"), (v5, "e")]:
+        f(k)
+
+    need(g, "g", "sr", 2 * NPAIR)
     others = [c for c in cores if c != core]
     fars = [c for c in others if not on_chip(c)]
     share = len(far_bits) // len(fars)
@@ -312,30 +203,27 @@ def rank_program(g, core, T, topo):
         else:
             i = fars.index(c)
             bits = far_bits[i * share:(i + 1) * share]
-        slot = (rank - T.rank_of(c)) % NR - 1
         trs.append(RemoteDMATransfer(dst_ids=[DstId(rid=rid, pnc=pid)], dma_engine_mask=sum(bits), remote_sem=sem.st,
-                                     src=T.L[:, 12:14], dst=T.L[:, 4 * slot:4 * slot + 2]))
+                                     src=T.L[:, slot:slot + 2 * NPAIR], dst=T.L[:, slot:slot + 2 * NPAIR]))
         n_st += len(bits)
     g.remote_dma_fused(trs, local_sem=sem.ls)
 
-    need(V, "v", "sr", 2)
+    need(V, "v", "sr", 2 * NPAIR)
     need(V, "v", "st", n_st)
-    vsync()
-    vop(tt(T.A2[:, 0:2], T.L[:, 0:16:8], T.L[:, 4:16:8], ADD))
-    vop(tt(T.M2[:, 0:2], T.L[:, 1:16:8], T.L[:, 5:16:8], MAX))
-    vsync()
-    vop(tt(T.TT[:, 0:1], T.A2[:, 0:1], T.A2[:, 1:2], ADD))
-    tt(T.SO[:, 1:2], T.M2[:, 0:1], T.M2[:, 1:2], MAX).then_inc(sem.so, 1)
-    vsync()
-    tt(T.SO[:, 0:1], T.TT[:, 0:1], T.CS[:, 0:1], MUL).then_inc(sem.so, 1)
+    nl = 2 * NPAIR * NR
+    V.tensor_reduce(T.SO[:, 0:1], T.L[:, 0:nl:2], X, ADD).then_inc(sem.so, 1)
+    V.tensor_reduce(T.SO[:, 1:2], T.L[:, 1:nl:2], X, MAX).then_inc(sem.so, 1)
 
-    for k in range(NCH):
-        a, b = ch[k]
-        need(SC, "a", "c%d" % k, 1)
-        SC.dma_start(T.y[:, a:b], T.Y[:, a:b]).then_inc(sem.yst, 16)
+    nst = 0
+    for k in "xyzwe":
+        need(SY, "s", "a4" + k)
+        for (s, e), _ in parts[k]:
+            h = s + HW if e <= HW else s - HW - 4
+            SY.dma_start(T.y[:, h:h + e - s], T.Y[:, s:e]).then_inc(sem.yst, 16)
+            nst += 1
     need(SY, "s", "so", 2)
     SY.dma_start(T.s[:, :], T.SO[:, :]).then_inc(sem.sd, 16)
 
     g.wait_ge(sem.ls, n_far + n_near + n_st)
-    g.wait_ge(sem.yst, 16 * NCH)
+    g.wait_ge(sem.yst, 16 * nst)
     g.wait_ge(sem.sd, 16)

@@ -35,6 +35,11 @@ for _k in "xyzw":
 SEMAPHORES = ([s + k for k in "xyzwe" for s in ("a1", "v1", "a2", "v2", "a3", "v3", "a4", "v4")]
               + list(UPC) + list(BPC) + ["bz", "hl", "hr", "sr", "st", "ls", "so", "sd", "yst"])
 
+A_ORDER = ["a1x", "a1y", "a2x", "a1z", "a2y", "a1w", "a2z", "a3x", "a2w", "a3e", "a3y", "a4x", "a3z", "a4y", "a3w", "a4z",
+           "a6x", "a4w", "a1e", "a6y", "a2e", "a6z", "a4e", "a6w", "a6e"]
+V_ORDER = ["v1x", "v1y", "v2x", "v1z", "v2y", "v1w", "v2z", "v3x", "v2w", "v3y", "v4x", "v3z", "v5x", "v4y", "v3w", "v4z",
+           "v5y", "v4w", "v1e", "v5z", "v2e", "v3e", "v5w", "v4e", "v5e"]
+
 
 def _bits(m):
     return [1 << i for i in range(m.bit_length()) if (m >> i) & 1]
@@ -85,7 +90,7 @@ def rank_program(g, core, T, topo):
         if HW < hi and lo < HW + 4:
             need(q, qn, "bz", 1)
 
-    for i, nm in enumerate(["uA", "uB", "bA", "bB", "uC", "uD", "bC", "bD"]):
+    for i, nm in enumerate(["uA", "uB", "uC", "uD", "bA", "bB", "bC", "bD"]):
         q = SY if i % 2 == 0 else A
         if nm in UPC:
             s, e, h = UPC[nm]
@@ -180,16 +185,11 @@ def rank_program(g, core, T, topo):
             c = slot + 2 * j + 1
             V.tensor_reduce(T.L[:, c:c + 1], T.D[:, s:e], X, MAX, apply_absolute_value=True).then_inc(sem.sr, 1)
 
-    for f, k in [(a1, "x"), (a1, "y"), (a2, "x"), (a2, "y"), (a3, "x"), (a3, "y"), (a3, "e"), (a4, "x"), (a4, "y"),
-                 (a6, "x"), (a6, "y"),
-                 (a1, "z"), (a1, "w"), (a2, "z"), (a2, "w"), (a3, "z"), (a3, "w"), (a4, "z"), (a4, "w"),
-                 (a1, "e"), (a6, "z"), (a2, "e"), (a6, "w"), (a4, "e"), (a6, "e")]:
-        f(k)
-    for f, k in [(v1, "x"), (v1, "y"), (v2, "x"), (v2, "y"), (v3, "x"), (v3, "y"), (v4, "x"), (v4, "y"),
-                 (v5, "x"), (v5, "y"),
-                 (v1, "z"), (v1, "w"), (v2, "z"), (v2, "w"), (v3, "z"), (v3, "w"), (v4, "z"), (v4, "w"),
-                 (v1, "e"), (v5, "z"), (v2, "e"), (v3, "e"), (v5, "w"), (v4, "e"), (v5, "e")]:
-        f(k)
+    steps = {"a1": a1, "a2": a2, "a3": a3, "a4": a4, "a6": a6, "v1": v1, "v2": v2, "v3": v3, "v4": v4, "v5": v5}
+    for o in A_ORDER:
+        steps[o[:2]](o[2])
+    for o in V_ORDER:
+        steps[o[:2]](o[2])
 
     need(g, "g", "sr", 2 * NPAIR)
     others = [c for c in cores if c != core]

@@ -7,38 +7,48 @@ HW = W // 2
 ZW = W + 8
 OW = W + 4
 ME = 32
-MAIN = (HW - ME) // 2
+SWD = 96
+MAIN = (HW - ME - SWD) // 2
+R0 = HW + 4 + ME
 
-CH = {"x": (MAIN, 2 * MAIN), "y": (HW + 4 + ME, HW + 4 + ME + MAIN), "z": (0, MAIN), "w": (HW + 4 + ME + MAIN, OW),
-      "e": (HW - ME, HW + 4 + ME)}
-POFF = {"x": 0, "y": 260, "z": 520, "w": 780, "e": 1040}
-UPC = {"uA": (MAIN, HW + 2, HW - 2 + MAIN), "uB": (HW + 6, HW + 8 + ME + MAIN, 0), "uC": (0, MAIN, HW - 2),
-       "uD": (HW + 8 + ME + MAIN, ZW, 2 + ME + MAIN)}
-BPC = {"bA": (MAIN, HW, HW + MAIN), "bB": (HW + 4, HW + 4 + ME + MAIN, 0), "bC": (0, MAIN, HW),
-       "bD": (HW + 4 + ME + MAIN, OW, ME + MAIN)}
-NPAIR = 6
+CH = {"z": (0, MAIN), "x": (MAIN, 2 * MAIN), "s": (2 * MAIN, HW - ME), "e": (HW - ME, R0),
+      "r": (R0, R0 + SWD), "y": (R0 + SWD, R0 + SWD + MAIN), "w": (R0 + SWD + MAIN, OW)}
+YE = CH["y"][1]
+POFF = {"x": 0, "y": 100, "z": 200, "w": 300, "e": 400}
+PE_O, TW_O = 104, 208
+UPC = {"uA": (MAIN, HW + 2, HW - 2 + MAIN), "uB": (HW + 6, YE + 4, 0), "uC": (0, MAIN, HW - 2),
+       "uD": (YE + 4, ZW, YE + 4 - HW - 6)}
+BPC = {"bA": (MAIN, HW, HW + MAIN), "bB": (HW + 4, YE, 0), "bC": (0, MAIN, HW), "bD": (YE, OW, YE - HW - 4)}
+NPAIR = 8
 
 SCRATCH = {
     "Z": ("sbuf", [128, ZW], "float32"),
     "B": ("sbuf", [128, OW], "float32"),
-    "P": ("sbuf", [128, 1120], "float32"),
+    "P": ("sbuf", [128, 440], "float32"),
+    "ZO": ("sbuf", [128, 440], "float32"),
+    "SJ": ("sbuf", [128, NPAIR * NR], "float32"),
     "Y": ("sbuf", [128, OW], "float32"),
     "D": ("sbuf", [128, OW], "float32"),
     "SQ": ("sbuf", [128, OW], "float32"),
     "L": ("sbuf", [128, 2 * NPAIR * NR], "float32"),
     "SO": ("sbuf", [128, 2], "float32"),
+    "C8": ("sbuf", [128, 128], "float32"), "C2": ("sbuf", [128, 128], "float32"),
+    "I8": ("sbuf", [128, 128], "float32"), "I2": ("sbuf", [128, 128], "float32"),
 }
-for _k in "xyzw":
-    SCRATCH["pu" + _k] = ("psum", [128, 512], "float32")
-    SCRATCH["pq" + _k] = ("psum", [128, 512], "float32")
+for _k in "xyzwe":
+    SCRATCH["pm" + _k] = ("psum", [128, 512], "float32")
+for _k in "sr":
+    SCRATCH["pt" + _k] = ("psum", [128, 512], "float32")
 
-SEMAPHORES = ([s + k for k in "xyzwe" for s in ("a1", "v1", "a2", "v2", "a3", "v3", "a4", "v4")]
-              + list(UPC) + list(BPC) + ["bz", "hl", "hr", "sr", "st", "ls", "so", "sd", "yst"])
+SEMAPHORES = ([s + k for k in "xyzwe" for s in ("a1", "v1", "v2", "a3", "v3", "a4", "v4")]
+              + [s + k for k in "sr" for s in ("t", "a4", "v4")]
+              + list(UPC) + list(BPC) + ["bz", "cm", "im", "hl", "hr", "sr", "st", "ls", "so", "sd", "yst"])
 
-A_ORDER = ["a1x", "a1y", "a2x", "a1z", "a2y", "a1w", "a2z", "a3x", "a2w", "a3e", "a3y", "a4x", "a3z", "a4y", "a3w", "a4z",
-           "a6x", "a4w", "a1e", "a6y", "a2e", "a6z", "a4e", "a6w", "a6e"]
-V_ORDER = ["v1x", "v1y", "v2x", "v1z", "v2y", "v1w", "v2z", "v3x", "v2w", "v3y", "v4x", "v3z", "v5x", "v4y", "v3w", "v4z",
-           "v5y", "v4w", "v1e", "v5z", "v2e", "v3e", "v5w", "v4e", "v5e"]
+A_ORDER = ["a1x", "a1y", "a1z", "a1w", "a3x", "a3y", "a6s", "a3z", "a6x", "a3w", "a4x", "a4s", "a6y", "a4y", "a3e", "a1e",
+           "a6z", "a4z", "a6w", "a6r", "a4w", "a4r", "a6e", "a4e"]
+V_ORDER = ["v1x", "v1y", "v2x", "v1z", "v2y", "v1w", "v2z", "v2w", "v3x", "v4s", "v4x", "v5s", "v3y", "v5x", "v4y", "v3z",
+           "v5y", "v4z", "v3w", "v5z", "v4w", "v1e", "v4r", "v2e", "v5w", "v3e", "v5r", "v4e", "v5e"]
+S_ORDER = "xsyzwre"
 
 
 def _bits(m):
@@ -49,7 +59,7 @@ def rank_program(g, core, T, topo):
     rank = T.rank_of(core)
     if rank is None:
         return
-    V, A, SY = g.vector, g.scalar, g.sync
+    V, A, SY, TE = g.vector, g.scalar, g.sync, g.tensor
     ADD, SUB, MAX = AluOpType.add, AluOpType.subtract, AluOpType.max
     COPY, SQUARE = ActivationFunctionType.Copy, ActivationFunctionType.Square
     X = AxisListType.X
@@ -98,7 +108,13 @@ def rank_program(g, core, T, topo):
         else:
             s, e, h = BPC[nm]
             q.dma_start(T.B[:, s:e], T.b[:, h:h + e - s]).then_inc(sem[nm], 16)
+
+    V.memset(T.C8[:, :], 0.125).then_inc(sem.cm, 1)
+    V.memset(T.C2[:, :], 0.5).then_inc(sem.cm, 1)
     V.memset(T.B[:, HW:HW + 4], 0.0).then_inc(sem.bz, 1)
+    g.wait_ge(sem.cm, 2)
+    g.affine_select(T.I8[:, :], T.C8[:, :], [[-1, 128]], AluOpType.is_equal, 0.0, 0, 1).then_inc(sem.im, 1)
+    g.affine_select(T.I2[:, :], T.C2[:, :], [[-1, 128]], AluOpType.is_equal, 0.0, 0, 1).then_inc(sem.im, 1)
 
     need(g, "g", "uA", 16)
     need(g, "g", "uB", 16)
@@ -113,79 +129,99 @@ def rank_program(g, core, T, topo):
                         halo(right, T.Z[:, HW:HW + 2], T.Z[:, HW + 4:HW + 6], "hl")],
                        local_sem=sem.ls)
 
-    def regs(k):
+    TE.wait_ge(sem.im, 2)
+    for k in "sr":
         a, b = CH[k]
         n = b - a
-        if k == "e":
-            up, pp, tw = T.pux[:, 264:264 + n + 3], T.pux[:, 336:336 + n], T.pux[:, 408:408 + n]
-        else:
-            up, pp, tw = T["pu" + k][:, 0:n + 3], T["pq" + k][:, 0:n], T["pq" + k][:, 256:256 + n]
-        return a, b, n, up, pp, tw, POFF[k]
+        need_z(TE, "t", a, a + n + 4)
+        for i, off in enumerate((0, 1, 3, 4)):
+            TE.matmul(T["pt" + k][:, 0:n], T.I8[:, :], T.Z[:, a + off:a + off + n], i == 0, False)
+        need_b(TE, "t", a, b)
+        TE.matmul(T["pt" + k][:, 0:n], T.I2[:, :], T.B[:, a:b], False, True).then_inc(sem["t" + k], 1)
+
+    NV4 = {k: (2 if k == "e" else 1) for k in CH}
 
     def a1(k):
-        a, b, n, up, pp, tw, po = regs(k)
-        need_z(A, "a", a, a + n + 3)
-        if k == "e":
-            need(A, "a", "v1x")
-            need(A, "a", "v4x")
-        A.activation(up, T.Z[:, a:a + n + 3], COPY).then_inc(sem["a1" + k], 1)
+        a, b = CH[k]
+        n = b - a
+        h, po = n // 2, POFF[k]
+        need_z(A, "a", a, a + n + 4)
+        A.activation(T["pm" + k][:, 0:h + 2], T.Z[:, a:a + n + 3:2], COPY, scale=0.125).then_inc(sem["a1" + k], 1)
+        A.activation(T.ZO[:, po:po + h + 2], T.Z[:, a + 1:a + n + 4:2], COPY, scale=0.125).then_inc(sem["a1" + k], 1)
 
     def v1(k):
-        a, b, n, up, pp, tw, po = regs(k)
-        need(V, "v", "a1" + k)
-        need_z(V, "v", a + 1, a + n + 4)
-        V.tensor_tensor(T.P[:, po:po + n + 3], up, T.Z[:, a + 1:a + n + 4], ADD).then_inc(sem["v1" + k], 1)
-
-    def a2(k):
-        a, b, n, up, pp, tw, po = regs(k)
-        need(A, "a", "v1" + k)
-        A.activation(pp, T.P[:, po:po + n], COPY).then_inc(sem["a2" + k], 1)
+        a, b = CH[k]
+        h, po, bank = (b - a) // 2, POFF[k], T["pm" + k]
+        need(V, "v", "a1" + k, 2)
+        V.tensor_tensor(bank[:, PE_O:PE_O + h + 2], bank[:, 0:h + 2], T.ZO[:, po:po + h + 2],
+                        ADD).then_inc(sem["v1" + k], 1)
+        V.tensor_tensor(T.P[:, po:po + h + 1], bank[:, 1:h + 2], T.ZO[:, po:po + h + 1],
+                        ADD).then_inc(sem["v1" + k], 1)
 
     def v2(k):
-        a, b, n, up, pp, tw, po = regs(k)
-        need(V, "v", "v1" + k)
-        need(V, "v", "a2" + k)
-        V.tensor_tensor(tw, pp, T.P[:, po + 3:po + n + 3], ADD).then_inc(sem["v2" + k], 1)
+        a, b = CH[k]
+        n, h, po, bank = b - a, (b - a) // 2, POFF[k], T["pm" + k]
+        need(V, "v", "v1" + k, 2)
+        V.tensor_tensor(bank[:, TW_O:TW_O + n:2], bank[:, PE_O:PE_O + h], T.P[:, po + 1:po + 1 + h],
+                        ADD).then_inc(sem["v2" + k], 1)
+        V.tensor_tensor(bank[:, TW_O + 1:TW_O + n:2], bank[:, PE_O + 2:PE_O + 2 + h], T.P[:, po:po + h],
+                        ADD).then_inc(sem["v2" + k], 1)
 
     def a3(k):
-        a, b, n, up, pp, tw, po = regs(k)
+        a, b = CH[k]
         need_b(A, "a", a, b)
-        A.activation(T.B[:, a:b], T.B[:, a:b], COPY, scale=4.0).then_inc(sem["a3" + k], 1)
+        A.activation(T.B[:, a:b], T.B[:, a:b], COPY, scale=0.5).then_inc(sem["a3" + k], 1)
 
     def v3(k):
-        a, b, n, up, pp, tw, po = regs(k)
-        need(V, "v", "v2" + k)
+        a, b = CH[k]
+        tw = T["pm" + k][:, TW_O:TW_O + b - a]
+        need(V, "v", "v2" + k, 2)
         need(V, "v", "a3" + k)
         V.tensor_tensor(tw, tw, T.B[:, a:b], ADD).then_inc(sem["v3" + k], 1)
 
     def a4(k):
-        a, b, n, up, pp, tw, po = regs(k)
-        need(A, "a", "v3" + k)
-        A.activation(T.Y[:, a:b], tw, COPY, scale=0.125).then_inc(sem["a4" + k], 1)
+        a, b = CH[k]
+        need(A, "a", "v4" + k, NV4[k])
+        src = T["pt" + k][:, 0:b - a] if k in "sr" else T["pm" + k][:, TW_O:TW_O + b - a]
+        A.activation(T.Y[:, a:b], src, COPY).then_inc(sem["a4" + k], 1)
 
     def v4(k):
-        a, b, n, up, pp, tw, po = regs(k)
-        need(V, "v", "a4" + k)
-        V.tensor_tensor(T.D[:, a:b], T.Y[:, a:b], up[:, 2:n + 2], SUB).then_inc(sem["v4" + k], 1)
+        a, b = CH[k]
+        if k in "sr":
+            need(V, "v", "t" + k)
+            need_z(V, "v", a + 2, b + 2)
+            V.tensor_tensor(T.D[:, a:b], T["pt" + k][:, 0:b - a], T.Z[:, a + 2:b + 2], SUB).then_inc(sem["v4" + k], 1)
+        elif k == "e":
+            need(V, "v", "v3" + k)
+            for o, dd in ((0, a), (ME + 4, a + ME)):
+                V.tensor_tensor(T.D[:, dd:dd + ME], T["pm" + k][:, TW_O + o:TW_O + o + ME], T.Z[:, a + o + 2:a + o + 2 + ME],
+                                SUB).then_inc(sem["v4" + k], 1)
+        else:
+            need(V, "v", "v3" + k)
+            need_z(V, "v", a + 2, b + 2)
+            V.tensor_tensor(T.D[:, a:b], T["pm" + k][:, TW_O:TW_O + b - a], T.Z[:, a + 2:b + 2], SUB).then_inc(sem["v4" + k], 1)
 
-    parts = {"x": [(CH["x"], 0)], "y": [(CH["y"], 1)], "z": [(CH["z"], 2)], "w": [(CH["w"], 3)],
-             "e": [((HW - ME, HW), 4), ((HW + 4, HW + 4 + ME), 5)]}
+    parts = {"x": [(CH["x"], 0)], "y": [(CH["y"], 1)], "z": [(CH["z"], 2)], "w": [(CH["w"], 3)], "s": [(CH["s"], 4)],
+             "r": [(CH["r"], 5)], "e": [((HW - ME, HW), 6), ((HW + 4, HW + 4 + ME), 7)]}
+    stat = dict(parts)
+    stat["e"] = [((HW - ME, HW + ME), 6)]
     slot = 2 * NPAIR * rank
+    V.memset(T.L[:, slot + 2 * NPAIR - 2:slot + 2 * NPAIR], 0.0).then_inc(sem.sr, 2)
 
     def a6(k):
-        need(A, "a", "v4" + k)
-        for (s, e), j in parts[k]:
+        need(A, "a", "v4" + k, NV4[k])
+        for (s, e), j in stat[k]:
             c = slot + 2 * j
             A.activation(T.SQ[:, s:e], T.D[:, s:e], SQUARE, scale=1.0 / 64.0,
                          accum_out=T.L[:, c:c + 1]).then_inc(sem.sr, 1)
 
     def v5(k):
-        need(V, "v", "v4" + k)
-        for (s, e), j in parts[k]:
+        need(V, "v", "v4" + k, NV4[k])
+        for (s, e), j in stat[k]:
             c = slot + 2 * j + 1
             V.tensor_reduce(T.L[:, c:c + 1], T.D[:, s:e], X, MAX, apply_absolute_value=True).then_inc(sem.sr, 1)
 
-    steps = {"a1": a1, "a2": a2, "a3": a3, "a4": a4, "a6": a6, "v1": v1, "v2": v2, "v3": v3, "v4": v4, "v5": v5}
+    steps = {"a1": a1, "a3": a3, "a4": a4, "a6": a6, "v1": v1, "v2": v2, "v3": v3, "v4": v4, "v5": v5}
     for o in A_ORDER:
         steps[o[:2]](o[2])
     for o in V_ORDER:
@@ -211,11 +247,13 @@ def rank_program(g, core, T, topo):
     need(V, "v", "sr", 2 * NPAIR)
     need(V, "v", "st", n_st)
     nl = 2 * NPAIR * NR
-    V.tensor_reduce(T.SO[:, 0:1], T.L[:, 0:nl:2], X, ADD).then_inc(sem.so, 1)
+    need(A, "a", "sr", 2 * NPAIR)
+    need(A, "a", "st", n_st)
+    A.activation(T.SJ[:, :], T.L[:, 0:nl:2], COPY, accum_out=T.SO[:, 0:1]).then_inc(sem.so, 1)
     V.tensor_reduce(T.SO[:, 1:2], T.L[:, 1:nl:2], X, MAX).then_inc(sem.so, 1)
 
     nst = 0
-    for k in "xyzwe":
+    for k in S_ORDER:
         need(SY, "s", "a4" + k)
         for (s, e), _ in parts[k]:
             h = s + HW if e <= HW else s - HW - 4

from concourse.bass import DstId, RemoteDMATransfer
from concourse.mybir import AluOpType, AxisListType, ActivationFunctionType

W = 1024
NR = 4
HW = W // 2
ZW = W + 8
OW = W + 4
ME = 32
SWD = 96
MAIN = (HW - ME - SWD) // 2
R0 = HW + 4 + ME

CH = {"z": (0, MAIN), "x": (MAIN, 2 * MAIN), "s": (2 * MAIN, HW - ME), "e": (HW - ME, R0),
      "r": (R0, R0 + SWD), "y": (R0 + SWD, R0 + SWD + MAIN), "w": (R0 + SWD + MAIN, OW)}
YE = CH["y"][1]
POFF = {"x": 0, "y": 100, "z": 200, "w": 300, "e": 400}
PE_O, TW_O = 104, 208
UPC = {"uA": (MAIN, HW + 2, HW - 2 + MAIN), "uB": (HW + 6, YE + 4, 0), "uC": (0, MAIN, HW - 2),
       "uD": (YE + 4, ZW, YE + 4 - HW - 6)}
BPC = {"bA": (MAIN, HW, HW + MAIN), "bB": (HW + 4, YE, 0), "bC": (0, MAIN, HW), "bD": (YE, OW, YE - HW - 4)}
NPAIR = 8

SCRATCH = {
    "Z": ("sbuf", [128, ZW], "float32"),
    "B": ("sbuf", [128, OW], "float32"),
    "P": ("sbuf", [128, 440], "float32"),
    "ZO": ("sbuf", [128, 440], "float32"),
    "SJ": ("sbuf", [128, NPAIR * NR], "float32"),
    "Y": ("sbuf", [128, OW], "float32"),
    "D": ("sbuf", [128, OW], "float32"),
    "SQ": ("sbuf", [128, OW], "float32"),
    "L": ("sbuf", [128, 2 * NPAIR * NR], "float32"),
    "SO": ("sbuf", [128, 2], "float32"),
    "C8": ("sbuf", [128, 128], "float32"), "C2": ("sbuf", [128, 128], "float32"),
    "I8": ("sbuf", [128, 128], "float32"), "I2": ("sbuf", [128, 128], "float32"),
}
for _k in "xyzwe":
    SCRATCH["pm" + _k] = ("psum", [128, 512], "float32")
for _k in "sr":
    SCRATCH["pt" + _k] = ("psum", [128, 512], "float32")

SEMAPHORES = ([s + k for k in "xyzwe" for s in ("a1", "v1", "v2", "a3", "v3", "a4", "v4")]
              + [s + k for k in "sr" for s in ("t", "a4", "v4")]
              + list(UPC) + list(BPC) + ["bz", "cm", "im", "hl", "hr", "sr", "st", "ls", "so", "sd", "yst"])

A_ORDER = ["a1x", "a1y", "a1z", "a1w", "a3x", "a3y", "a6s", "a3z", "a6x", "a3w", "a4x", "a4s", "a6y", "a4y", "a3e", "a1e",
           "a6z", "a4z", "a6w", "a6r", "a4w", "a4r", "a6e", "a4e"]
V_ORDER = ["v1x", "v1y", "v2x", "v1z", "v2y", "v1w", "v2z", "v2w", "v3x", "v4s", "v4x", "v5s", "v3y", "v5x", "v4y", "v3z",
           "v5y", "v4z", "v3w", "v5z", "v4w", "v1e", "v4r", "v2e", "v5w", "v3e", "v5r", "v4e", "v5e"]
S_ORDER = "xsyzwre"


def _bits(m):
    return [1 << i for i in range(m.bit_length()) if (m >> i) & 1]


def rank_program(g, core, T, topo):
    rank = T.rank_of(core)
    if rank is None:
        return
    V, A, SY, TE = g.vector, g.scalar, g.sync, g.tensor
    ADD, SUB, MAX = AluOpType.add, AluOpType.subtract, AluOpType.max
    COPY, SQUARE = ActivationFunctionType.Copy, ActivationFunctionType.Square
    X = AxisListType.X
    sem = T.sem
    cores = list(T.cores)
    left, right = cores[(rank - 1) % NR], cores[(rank + 1) % NR]

    def on_chip(c):
        return topo.host(c) == topo.host(core) and topo.chip(c) == topo.chip(core)

    assert on_chip(left) != on_chip(right)
    near, far = (left, right) if on_chip(left) else (right, left)

    far_bits = _bits(topo.mask(core, far))
    near_bits = [x for x in _bits(topo.mask(core, near)) if x not in far_bits][:4]
    n_far, n_near = len(far_bits), len(near_bits)

    seen = set()

    def need(q, qn, name, val=1):
        if (qn, name) not in seen:
            q.wait_ge(sem[name], val)
            seen.add((qn, name))

    def need_z(q, qn, lo, hi):
        for nm, (s, e, _) in UPC.items():
            if s < hi and lo < e:
                need(q, qn, nm, 16)
        if HW + 2 < hi and lo < HW + 4:
            need(q, qn, "hr", n_near if on_chip(right) else n_far)
        if HW + 4 < hi and lo < HW + 6:
            need(q, qn, "hl", n_near if on_chip(left) else n_far)

    def need_b(q, qn, lo, hi):
        for nm, (s, e, _) in BPC.items():
            if s < hi and lo < e:
                need(q, qn, nm, 16)
        if HW < hi and lo < HW + 4:
            need(q, qn, "bz", 1)

    for i, nm in enumerate(["uA", "uB", "uC", "uD", "bA", "bB", "bC", "bD"]):
        q = SY if i % 2 == 0 else A
        if nm in UPC:
            s, e, h = UPC[nm]
            q.dma_start(T.Z[:, s:e], T.u[:, h:h + e - s]).then_inc(sem[nm], 16)
        else:
            s, e, h = BPC[nm]
            q.dma_start(T.B[:, s:e], T.b[:, h:h + e - s]).then_inc(sem[nm], 16)

    V.memset(T.C8[:, :], 0.125).then_inc(sem.cm, 1)
    V.memset(T.C2[:, :], 0.5).then_inc(sem.cm, 1)
    V.memset(T.B[:, HW:HW + 4], 0.0).then_inc(sem.bz, 1)
    g.wait_ge(sem.cm, 2)
    g.affine_select(T.I8[:, :], T.C8[:, :], [[-1, 128]], AluOpType.is_equal, 0.0, 0, 1).then_inc(sem.im, 1)
    g.affine_select(T.I2[:, :], T.C2[:, :], [[-1, 128]], AluOpType.is_equal, 0.0, 0, 1).then_inc(sem.im, 1)

    need(g, "g", "uA", 16)
    need(g, "g", "uB", 16)

    def halo(dst_core, src, dst, name):
        rid, pid = topo.addr(dst_core, core)
        return RemoteDMATransfer(dst_ids=[DstId(rid=rid, pnc=pid)],
                                 dma_engine_mask=sum(near_bits if on_chip(dst_core) else far_bits),
                                 remote_sem=sem[name], src=src, dst=dst)

    g.remote_dma_fused([halo(left, T.Z[:, HW + 6:HW + 8], T.Z[:, HW + 2:HW + 4], "hr"),
                        halo(right, T.Z[:, HW:HW + 2], T.Z[:, HW + 4:HW + 6], "hl")],
                       local_sem=sem.ls)

    TE.wait_ge(sem.im, 2)
    for k in "sr":
        a, b = CH[k]
        n = b - a
        need_z(TE, "t", a, a + n + 4)
        for i, off in enumerate((0, 1, 3, 4)):
            TE.matmul(T["pt" + k][:, 0:n], T.I8[:, :], T.Z[:, a + off:a + off + n], i == 0, False)
        need_b(TE, "t", a, b)
        TE.matmul(T["pt" + k][:, 0:n], T.I2[:, :], T.B[:, a:b], False, True).then_inc(sem["t" + k], 1)

    NV4 = {k: (2 if k == "e" else 1) for k in CH}

    def a1(k):
        a, b = CH[k]
        n = b - a
        h, po = n // 2, POFF[k]
        need_z(A, "a", a, a + n + 4)
        A.activation(T["pm" + k][:, 0:h + 2], T.Z[:, a:a + n + 3:2], COPY, scale=0.125).then_inc(sem["a1" + k], 1)
        A.activation(T.ZO[:, po:po + h + 2], T.Z[:, a + 1:a + n + 4:2], COPY, scale=0.125).then_inc(sem["a1" + k], 1)

    def v1(k):
        a, b = CH[k]
        h, po, bank = (b - a) // 2, POFF[k], T["pm" + k]
        need(V, "v", "a1" + k, 2)
        V.tensor_tensor(bank[:, PE_O:PE_O + h + 2], bank[:, 0:h + 2], T.ZO[:, po:po + h + 2],
                        ADD).then_inc(sem["v1" + k], 1)
        V.tensor_tensor(T.P[:, po:po + h + 1], bank[:, 1:h + 2], T.ZO[:, po:po + h + 1],
                        ADD).then_inc(sem["v1" + k], 1)

    def v2(k):
        a, b = CH[k]
        n, h, po, bank = b - a, (b - a) // 2, POFF[k], T["pm" + k]
        need(V, "v", "v1" + k, 2)
        V.tensor_tensor(bank[:, TW_O:TW_O + n:2], bank[:, PE_O:PE_O + h], T.P[:, po + 1:po + 1 + h],
                        ADD).then_inc(sem["v2" + k], 1)
        V.tensor_tensor(bank[:, TW_O + 1:TW_O + n:2], bank[:, PE_O + 2:PE_O + 2 + h], T.P[:, po:po + h],
                        ADD).then_inc(sem["v2" + k], 1)

    def a3(k):
        a, b = CH[k]
        need_b(A, "a", a, b)
        A.activation(T.B[:, a:b], T.B[:, a:b], COPY, scale=0.5).then_inc(sem["a3" + k], 1)

    def v3(k):
        a, b = CH[k]
        tw = T["pm" + k][:, TW_O:TW_O + b - a]
        need(V, "v", "v2" + k, 2)
        need(V, "v", "a3" + k)
        V.tensor_tensor(tw, tw, T.B[:, a:b], ADD).then_inc(sem["v3" + k], 1)

    def a4(k):
        a, b = CH[k]
        need(A, "a", "v4" + k, NV4[k])
        src = T["pt" + k][:, 0:b - a] if k in "sr" else T["pm" + k][:, TW_O:TW_O + b - a]
        A.activation(T.Y[:, a:b], src, COPY).then_inc(sem["a4" + k], 1)

    def v4(k):
        a, b = CH[k]
        if k in "sr":
            need(V, "v", "t" + k)
            need_z(V, "v", a + 2, b + 2)
            V.tensor_tensor(T.D[:, a:b], T["pt" + k][:, 0:b - a], T.Z[:, a + 2:b + 2], SUB).then_inc(sem["v4" + k], 1)
        elif k == "e":
            need(V, "v", "v3" + k)
            for o, dd in ((0, a), (ME + 4, a + ME)):
                V.tensor_tensor(T.D[:, dd:dd + ME], T["pm" + k][:, TW_O + o:TW_O + o + ME], T.Z[:, a + o + 2:a + o + 2 + ME],
                                SUB).then_inc(sem["v4" + k], 1)
        else:
            need(V, "v", "v3" + k)
            need_z(V, "v", a + 2, b + 2)
            V.tensor_tensor(T.D[:, a:b], T["pm" + k][:, TW_O:TW_O + b - a], T.Z[:, a + 2:b + 2], SUB).then_inc(sem["v4" + k], 1)

    parts = {"x": [(CH["x"], 0)], "y": [(CH["y"], 1)], "z": [(CH["z"], 2)], "w": [(CH["w"], 3)], "s": [(CH["s"], 4)],
             "r": [(CH["r"], 5)], "e": [((HW - ME, HW), 6), ((HW + 4, HW + 4 + ME), 7)]}
    stat = dict(parts)
    stat["e"] = [((HW - ME, HW + ME), 6)]
    slot = 2 * NPAIR * rank
    V.memset(T.L[:, slot + 2 * NPAIR - 2:slot + 2 * NPAIR], 0.0).then_inc(sem.sr, 2)

    def a6(k):
        need(A, "a", "v4" + k, NV4[k])
        for (s, e), j in stat[k]:
            c = slot + 2 * j
            A.activation(T.SQ[:, s:e], T.D[:, s:e], SQUARE, scale=1.0 / 64.0,
                         accum_out=T.L[:, c:c + 1]).then_inc(sem.sr, 1)

    def v5(k):
        need(V, "v", "v4" + k, NV4[k])
        for (s, e), j in stat[k]:
            c = slot + 2 * j + 1
            V.tensor_reduce(T.L[:, c:c + 1], T.D[:, s:e], X, MAX, apply_absolute_value=True).then_inc(sem.sr, 1)

    steps = {"a1": a1, "a3": a3, "a4": a4, "a6": a6, "v1": v1, "v2": v2, "v3": v3, "v4": v4, "v5": v5}
    for o in A_ORDER:
        steps[o[:2]](o[2])
    for o in V_ORDER:
        steps[o[:2]](o[2])

    need(g, "g", "sr", 2 * NPAIR)
    others = [c for c in cores if c != core]
    fars = [c for c in others if not on_chip(c)]
    share = len(far_bits) // len(fars)
    trs, n_st = [], 0
    for c in others:
        rid, pid = topo.addr(c, core)
        if on_chip(c):
            bits = near_bits
        else:
            i = fars.index(c)
            bits = far_bits[i * share:(i + 1) * share]
        trs.append(RemoteDMATransfer(dst_ids=[DstId(rid=rid, pnc=pid)], dma_engine_mask=sum(bits), remote_sem=sem.st,
                                     src=T.L[:, slot:slot + 2 * NPAIR], dst=T.L[:, slot:slot + 2 * NPAIR]))
        n_st += len(bits)
    g.remote_dma_fused(trs, local_sem=sem.ls)

    need(V, "v", "sr", 2 * NPAIR)
    need(V, "v", "st", n_st)
    nl = 2 * NPAIR * NR
    need(A, "a", "sr", 2 * NPAIR)
    need(A, "a", "st", n_st)
    A.activation(T.SJ[:, :], T.L[:, 0:nl:2], COPY, accum_out=T.SO[:, 0:1]).then_inc(sem.so, 1)
    V.tensor_reduce(T.SO[:, 1:2], T.L[:, 1:nl:2], X, MAX).then_inc(sem.so, 1)

    nst = 0
    for k in S_ORDER:
        need(SY, "s", "a4" + k)
        for (s, e), _ in parts[k]:
            h = s + HW if e <= HW else s - HW - 4
            SY.dma_start(T.y[:, h:h + e - s], T.Y[:, s:e]).then_inc(sem.yst, 16)
            nst += 1
    need(SY, "s", "so", 2)
    SY.dma_start(T.s[:, :], T.SO[:, :]).then_inc(sem.sd, 16)

    g.wait_ge(sem.ls, n_far + n_near + n_st)
    g.wait_ge(sem.yst, 16 * nst)
    g.wait_ge(sem.sd, 16)
